import numpy as np
import ml_dtypes


def mxq(x, axis, fmt="e4m3"):
    dtype, down = {"e4m3": (ml_dtypes.float8_e4m3fn, 7), "e5m2": (ml_dtypes.float8_e5m2, 14)}[fmt]
    v = np.moveaxis(np.asarray(x, np.float32).astype(ml_dtypes.bfloat16).astype(np.float64), axis, -1)
    blocks = v.reshape(v.shape[:-1] + (-1, 32))
    amax = np.abs(blocks).max(-1, keepdims=True)
    byte = np.maximum(np.where(amax > 0, np.frexp(amax)[1] - 1 + 127, 0) - down, 1)
    scale = np.exp2(byte - 127.0)
    codes = (blocks / scale).astype(np.float32).astype(dtype).astype(np.float64)
    return np.moveaxis((codes * scale).reshape(v.shape), -1, axis)


WIDE = False


def mx_kscale(k):
    if not WIDE:
        return np.ones(k)
    levels = np.array([10, -10, 5, -5, 0])
    if k % 512:
        return np.exp2(np.random.permutation(np.resize(levels, k // 32))).repeat(32)
    a = np.empty((k // 512, 16))
    for p in range(k // 512):
        a[p, :8] = np.random.permutation(np.resize(levels, 8))
        for g in range(8):
            far = levels[np.abs(levels - a[p, g]) >= 10]
            a[p, g + 8] = far[np.random.randint(len(far))]
    return np.exp2(a.ravel()).repeat(32)


def f64(x):
    return np.asarray(x).astype(np.float64)


def striped(idx):
    return np.tile(idx.reshape(-1, 16).T, (8, 1)).astype(np.uint16)


def unstriped(offs):
    return offs[:16].T.reshape(-1).astype(np.int64)


def pack_weight(w):
    k, n = w.shape
    w = f64(np.asarray(w, np.float32).astype(ml_dtypes.bfloat16)).reshape(k // 32, 32, n)
    amax = np.abs(w).max(1)
    byte = np.clip(np.where(amax > 0, np.frexp(amax)[1] - 1 + 127 - 7, 1), 1, 254)
    scaled = (w * np.exp2(127.0 - byte)[:, None, :]).reshape(k, n).astype(np.float32)
    words = np.ascontiguousarray(scaled.reshape(k // 512, 128, 4, n).transpose(0, 1, 3, 2)).astype(ml_dtypes.float8_e4m3fn).view(np.uint8)
    return words, np.ascontiguousarray(byte.astype(np.uint8).reshape(k // 512, 16, n))


def unpack_weight(words, scales):
    g, p, n, _ = words.shape
    vals = np.ascontiguousarray(words).view(ml_dtypes.float8_e4m3fn).astype(np.float64) * np.repeat(np.exp2(scales.astype(np.float64) - 127.0), 8, axis=1)[..., None]
    return vals.transpose(0, 1, 3, 2).reshape(g * 512, n)


def gelu(v):
    return 0.5 * v * (1.0 + np.tanh(np.sqrt(2.0 / np.pi) * (v + 0.044715 * v**3)))


K, T, D, S, V, R, N = 512, 4096, 3, 1536, 512, 8, 512


def setup_inputs():
    n = np.random.standard_normal
    s = mx_kscale(K)[:, None]
    packed = pack_weight(n((K, T)) * s)
    return {
        "x_words": packed[0],
        "x_scales": packed[1],
        "w": (n((D, K, N)) / np.sqrt(D * K) / s[None]).astype(np.float32),
        "b": (0.3 * n((N, 1))).astype(np.float32),
        "offs": striped(np.concatenate([R * np.arange(V) + np.random.randint(0, R, V) for _ in range(D)])),
    }


def reference(x_words, x_scales, w, b, offs):
    idx = unstriped(offs)
    xq = unpack_weight(x_words, x_scales)[:, idx]
    wq = mxq(f64(w), 1, "e4m3")
    y = sum(wq[d].T @ xq[:, d * V:(d + 1) * V] for d in range(D))
    y = gelu(y + f64(b))
    return y

@@ -1,0 +1,129 @@
+from contextlib import ExitStack
+
+import concourse.mybir as mybir
+from concourse.masks import make_identity
+
+K, T, TAPS, V, M = 512, 4096, 3, 512, 512
+FLOPS = 2 * TAPS * K * M * V
+
+F32 = mybir.dt.float32
+BF16 = mybir.dt.bfloat16
+I32 = mybir.dt.int32
+U32 = mybir.dt.uint32
+U16 = mybir.dt.uint16
+U8 = mybir.dt.uint8
+FP8X4 = mybir.dt.float8_e4m3fn_x4
+GELU = mybir.ActivationFunctionType.Gelu_apprx_tanh
+
+P = 128
+PACK = 4
+LINE = 4
+STRIPE = 16
+M_TILE = 128
+
+
+def tile_picked_deform_lin_gelu_def_p_kernel(tc, x_words, x_scales, w, b, offs, out):
+    nc = tc.nc
+    with ExitStack() as ctx:
+        keep = ctx.enter_context(tc.tile_pool(name="keep", bufs=1))
+        psum = ctx.enter_context(tc.psum_pool(name="psum", bufs=1))
+
+        offsets = keep.tile([P, TAPS * V // STRIPE], U16, name="offsets")
+        nc.sync.dma_start(offsets[:], offs)
+
+        word_table = keep.tile([P, T], U32, name="word_table", align_bytes=64)
+        words_in = x_words[0].rearrange("p n t -> p (n t)")
+
+        def load_words(c0, c1):
+            nc.sync.dma_start(word_table[:, c0:c1].bitcast(I32), words_in[:, PACK * c0 : PACK * c1].bitcast(I32))
+
+        H = T // 2
+        scale_table = keep.tile([P, T], U8, name="scale_table", align_bytes=64)
+        nc.vector.memset(scale_table[:].bitcast(I32), 0)
+        load_words(0, 1024)
+        for q in range(4):
+            nc.sync.dma_start(
+                scale_table[32 * q : 32 * q + 4, :].bitcast(I32),
+                x_scales[0, 4 * q : 4 * q + 4, :].bitcast(I32),
+            )
+        load_words(1024, H)
+        load_words(H, T)
+
+        ident = keep.tile([P, P], F32, name="ident")
+        make_identity(nc, ident[:])
+        warm = keep.tile([P, 1], F32, name="warm")
+        nc.scalar.activation(warm[:], ident[:, 0:1], GELU)
+        bias_rows = keep.tile([P, P], F32, name="bias_rows")
+        nc.gpsimd.memset(bias_rows[:], 0.0)
+        nc.gpsimd.dma_start(bias_rows[0 : M // M_TILE, :], b.rearrange("(t p) o -> t (p o)", p=P))
+        bias_ps = psum.tile([P, P], F32, name="bias_ps")
+        nc.tensor.transpose(bias_ps[:], bias_rows[:], ident[:])
+        bias = keep.tile([P, M // M_TILE], F32, name="bias")
+        nc.scalar.copy(bias[:], bias_ps[:, 0 : M // M_TILE])
+
+        pieces = [(0, 0, 256), (0, 256, 256), (1, 0, 256), (1, 256, 256)] + [(2, m0, M_TILE) for m0 in range(0, M, M_TILE)]
+        raw = []
+        for i, (d, m0, width) in enumerate(pieces):
+            r = keep.tile([P, PACK, width], F32, name=f"raw{i}")
+            nc.sync.dma_start(r[:], w[d].rearrange("(p j) m -> p j m", j=PACK)[:, :, m0 : m0 + width])
+            raw.append(r)
+
+        x_codes = keep.tile([P, TAPS * V], U32, name="x_codes", align_bytes=64)
+        x_bytes = keep.tile([P, TAPS * V], U8, name="x_bytes", align_bytes=64)
+
+        def gather(dst, table, e0, e1, cols):
+            nc.vector.tensor_copy(dst[:, e0:e1], table[:, 0:cols].indirect(offsets[:, e0 // STRIPE : e1 // STRIPE]))
+
+        for d in range(TAPS):
+            gather(x_bytes, scale_table, d * V, (d + 1) * V, T)
+        gather(x_codes, word_table, 0, V // 2, T // 2)
+        gather(x_codes, word_table, V // 2, V + V // 2, T)
+        gather(x_codes, word_table, V + V // 2, TAPS * V, T)
+
+        w_codes = keep.tile([P, TAPS * M], U32, name="w_codes", align_bytes=64)
+        w_bytes = keep.tile([P, TAPS * M], U8, name="w_bytes", align_bytes=64)
+        groups = [(0, 0, V), (1, 0, V), (2, 0, V), (3, 0, V // 2), (3, V // 2, V // 2)]
+        ys = [keep.tile([P, V], F32, name=f"y{t}") for t in range(M // M_TILE)]
+        acc = [psum.tile([P, g[2]], F32, name=f"acc{i}", tag=f"acc{i}") for i, g in enumerate(groups)]
+        grouped = [keep.tile([P, width, PACK], BF16, name=f"grouped{i}", align_bytes=64) for i, (d, m0, width) in enumerate(pieces)]
+
+        def cast(i):
+            dst = grouped[i][:].rearrange("p (c i) t -> p c t i", i=LINE)
+            src = raw[i][:].rearrange("p t (c i) -> p c t i", i=LINE)
+            if i < 4:
+                nc.scalar.copy(dst, src)
+            else:
+                nc.vector.tensor_copy(dst, src)
+
+        def multiply(i):
+            d, m0, width = pieces[i]
+            cols = slice(d * M + m0, d * M + m0 + width)
+            nc.vector.quantize_mx(
+                out=w_codes[:, cols].bitcast(FP8X4),
+                scales=w_bytes[:, cols],
+                in_=grouped[i][:].rearrange("p m t -> p (m t)"),
+            )
+            for g, (t, v0, n) in enumerate(groups):
+                if not m0 <= t * M_TILE < m0 + width:
+                    continue
+                mc = slice(d * M + t * M_TILE, d * M + (t + 1) * M_TILE)
+                vc = slice(d * V + v0, d * V + v0 + n)
+                nc.tensor.matmul_mx(
+                    out=acc[g][:],
+                    lhsT=w_codes[:, mc].bitcast(FP8X4),
+                    lhsT_scale=w_bytes[:, mc],
+                    rhs=x_codes[:, vc].bitcast(FP8X4),
+                    rhs_scale=x_bytes[:, vc],
+                    start=(d == 0),
+                    stop=(d == TAPS - 1),
+                )
+                if d == TAPS - 1:
+                    y = ys[t]
+                    nc.scalar.activation(y[:, v0 : v0 + n], acc[g][:], GELU, bias=bias[:, t : t + 1])
+                    nc.sync.dma_start(out[t * M_TILE : (t + 1) * M_TILE, v0 : v0 + n], y[:, v0 : v0 + n])
+
+        cast(0)
+        for i in range(1, len(pieces)):
+            cast(i)
+            multiply(i - 1)
+        multiply(len(pieces) - 1)

@@ -20,6 +20,9 @@ PACK = 4
 LINE = 4
 STRIPE = 16
 M_TILE = 128
+PLANE = 4
+EARLY = 384
+SCALAR_PIECES = 4
 
 
 def tile_picked_deform_lin_gelu_def_p_kernel(tc, x_words, x_scales, w, b, offs, out):
@@ -31,71 +34,60 @@ def tile_picked_deform_lin_gelu_def_p_kernel(tc, x_words, x_scales, w, b, offs, 
         offsets = keep.tile([P, TAPS * V // STRIPE], U16, name="offsets")
         nc.sync.dma_start(offsets[:], offs)
 
+        pieces = [(0, 0, 256), (1, 0, 256), (2, 0, 256), (0, 256, 256), (1, 256, 128), (2, 256, 128), (1, 384, 128), (2, 384, 128)]
+        raw = [keep.tile([P, PACK, width], F32, name=f"raw{i}") for i, (d, m0, width) in enumerate(pieces)]
+
+        def load_piece(i):
+            d, m0, width = pieces[i]
+            nc.sync.dma_start(raw[i][:], w[d].rearrange("(p j) m -> p j m", j=PACK)[:, :, m0 : m0 + width])
+
         word_table = keep.tile([P, T], U32, name="word_table", align_bytes=64)
         words_in = x_words[0].rearrange("p n t -> p (n t)")
 
         def load_words(c0, c1):
             nc.sync.dma_start(word_table[:, c0:c1].bitcast(I32), words_in[:, PACK * c0 : PACK * c1].bitcast(I32))
 
-        H = T // 2
         scale_table = keep.tile([P, T], U8, name="scale_table", align_bytes=64)
         nc.vector.memset(scale_table[:].bitcast(I32), 0)
-        load_words(0, 1024)
-        for q in range(4):
-            nc.sync.dma_start(
-                scale_table[32 * q : 32 * q + 4, :].bitcast(I32),
-                x_scales[0, 4 * q : 4 * q + 4, :].bitcast(I32),
-            )
-        load_words(1024, H)
-        load_words(H, T)
+        warm = keep.tile([P, 2], F32, name="warm")
+        nc.gpsimd.memset(warm[:, 0:1], 0.0)
+        nc.scalar.activation(warm[:, 1:2], warm[:, 0:1], GELU)
+        bias_rows = keep.tile([P, P], F32, name="bias_rows")
+        nc.gpsimd.memset(bias_rows[:], 0.0)
+        load_piece(0)
+        nc.sync.dma_start(scale_table[0:P:8, :].bitcast(I32), x_scales[0].bitcast(I32))
+        nc.sync.dma_start(bias_rows[0 : M // M_TILE, :], b.rearrange("(t p) o -> t (p o)", p=P))
+        load_words(0, 8 * EARLY)
+        load_words(8 * EARLY, T)
 
         ident = keep.tile([P, P], F32, name="ident")
         make_identity(nc, ident[:])
-        warm = keep.tile([P, 1], F32, name="warm")
-        nc.scalar.activation(warm[:], ident[:, 0:1], GELU)
-        bias_rows = keep.tile([P, P], F32, name="bias_rows")
-        nc.gpsimd.memset(bias_rows[:], 0.0)
-        nc.gpsimd.dma_start(bias_rows[0 : M // M_TILE, :], b.rearrange("(t p) o -> t (p o)", p=P))
-        bias_ps = psum.tile([P, P], F32, name="bias_ps")
-        nc.tensor.transpose(bias_ps[:], bias_rows[:], ident[:])
-        bias = keep.tile([P, M // M_TILE], F32, name="bias")
-        nc.scalar.copy(bias[:], bias_ps[:, 0 : M // M_TILE])
-
-        pieces = [(0, 0, 256), (0, 256, 256), (1, 0, 256), (1, 256, 256)] + [(2, m0, M_TILE) for m0 in range(0, M, M_TILE)]
-        raw = []
-        for i, (d, m0, width) in enumerate(pieces):
-            r = keep.tile([P, PACK, width], F32, name=f"raw{i}")
-            nc.sync.dma_start(r[:], w[d].rearrange("(p j) m -> p j m", j=PACK)[:, :, m0 : m0 + width])
-            raw.append(r)
+        for i in range(1, len(pieces)):
+            load_piece(i)
 
         x_codes = keep.tile([P, TAPS * V], U32, name="x_codes", align_bytes=64)
+        picked_bytes = keep.tile([P, TAPS * V], U8, name="picked_bytes", align_bytes=64)
         x_bytes = keep.tile([P, TAPS * V], U8, name="x_bytes", align_bytes=64)
+        nc.gpsimd.memset(x_bytes[:].bitcast(I32), 0)
 
         def gather(dst, table, e0, e1, cols):
             nc.vector.tensor_copy(dst[:, e0:e1], table[:, 0:cols].indirect(offsets[:, e0 // STRIPE : e1 // STRIPE]))
 
-        for d in range(TAPS):
-            gather(x_bytes, scale_table, d * V, (d + 1) * V, T)
-        gather(x_codes, word_table, 0, V // 2, T // 2)
-        gather(x_codes, word_table, V // 2, V + V // 2, T)
-        gather(x_codes, word_table, V + V // 2, TAPS * V, T)
-
         w_codes = keep.tile([P, TAPS * M], U32, name="w_codes", align_bytes=64)
         w_bytes = keep.tile([P, TAPS * M], U8, name="w_bytes", align_bytes=64)
-        groups = [(0, 0, V), (1, 0, V), (2, 0, V), (3, 0, V // 2), (3, V // 2, V // 2)]
+        groups = [(t, v0, V // 2) for v0 in (0, V // 2) for t in range(M // M_TILE)]
         ys = [keep.tile([P, V], F32, name=f"y{t}") for t in range(M // M_TILE)]
-        acc = [psum.tile([P, g[2]], F32, name=f"acc{i}", tag=f"acc{i}") for i, g in enumerate(groups)]
         grouped = [keep.tile([P, width, PACK], BF16, name=f"grouped{i}", align_bytes=64) for i, (d, m0, width) in enumerate(pieces)]
 
         def cast(i):
             dst = grouped[i][:].rearrange("p (c i) t -> p c t i", i=LINE)
             src = raw[i][:].rearrange("p t (c i) -> p c t i", i=LINE)
-            if i < 4:
+            if i < SCALAR_PIECES:
                 nc.scalar.copy(dst, src)
             else:
                 nc.vector.tensor_copy(dst, src)
 
-        def multiply(i):
+        def quantize(i):
             d, m0, width = pieces[i]
             cols = slice(d * M + m0, d * M + m0 + width)
             nc.vector.quantize_mx(
@@ -103,7 +95,10 @@ def tile_picked_deform_lin_gelu_def_p_kernel(tc, x_words, x_scales, w, b, offs, 
                 scales=w_bytes[:, cols],
                 in_=grouped[i][:].rearrange("p m t -> p (m t)"),
             )
-            for g, (t, v0, n) in enumerate(groups):
+
+        def multiply(i):
+            d, m0, width = pieces[i]
+            for g, (t, v0, n) in sorted(enumerate(groups), key=lambda e: e[1] if d > 0 else e[0]):
                 if not m0 <= t * M_TILE < m0 + width:
                     continue
                 mc = slice(d * M + t * M_TILE, d * M + (t + 1) * M_TILE)
@@ -113,17 +108,38 @@ def tile_picked_deform_lin_gelu_def_p_kernel(tc, x_words, x_scales, w, b, offs, 
                     lhsT=w_codes[:, mc].bitcast(FP8X4),
                     lhsT_scale=w_bytes[:, mc],
                     rhs=x_codes[:, vc].bitcast(FP8X4),
-                    rhs_scale=x_bytes[:, vc],
+                    rhs_scale=x_bytes[PLANE:P, vc],
                     start=(d == 0),
                     stop=(d == TAPS - 1),
                 )
                 if d == TAPS - 1:
                     y = ys[t]
                     nc.scalar.activation(y[:, v0 : v0 + n], acc[g][:], GELU, bias=bias[:, t : t + 1])
-                    nc.sync.dma_start(out[t * M_TILE : (t + 1) * M_TILE, v0 : v0 + n], y[:, v0 : v0 + n])
+                    if t == M // M_TILE - 1:
+                        nc.sync.dma_start(out[t * M_TILE : (t + 1) * M_TILE, v0 : v0 + n], y[:, v0 : v0 + n])
+                    elif v0 > 0:
+                        nc.sync.dma_start(out[t * M_TILE : (t + 1) * M_TILE, :], y[:])
+
+        bias_ps = psum.tile([P, P], F32, name="bias_ps", tag="acc7")
+        nc.tensor.transpose(bias_ps[:], bias_rows[:], ident[:])
+        bias = keep.tile([P, M // M_TILE], F32, name="bias")
+        nc.scalar.copy(bias[:], bias_ps[:, 0 : M // M_TILE])
+        acc = [psum.tile([P, g[2]], F32, name=f"acc{i}", tag=f"acc{i}") for i, g in enumerate(groups)]
 
         cast(0)
-        for i in range(1, len(pieces)):
+        gather(picked_bytes, scale_table, 0, TAPS * V, T)
+        for r in range(4):
+            nc.scalar.dma_start(x_bytes[PLANE + r : P : 32, :].bitcast(I32), picked_bytes[8 * r : P : 32, :].bitcast(I32))
+        quantize(0)
+        gather(x_codes, word_table, 0, EARLY, 8 * EARLY)
+        gather(x_codes, word_table, EARLY, EARLY + V, T)
+        gather(x_codes, word_table, EARLY + V, 3 * V, T)
+        multiply(0)
+
+        cast(1)
+        for i in range(2, len(pieces)):
             cast(i)
+            quantize(i - 1)
             multiply(i - 1)
+        quantize(len(pieces) - 1)
         multiply(len(pieces) - 1)

from contextlib import ExitStack

import concourse.mybir as mybir
from concourse.masks import make_identity

K, T, TAPS, V, M = 512, 4096, 3, 512, 512
FLOPS = 2 * TAPS * K * M * V

F32 = mybir.dt.float32
BF16 = mybir.dt.bfloat16
I32 = mybir.dt.int32
U32 = mybir.dt.uint32
U16 = mybir.dt.uint16
U8 = mybir.dt.uint8
FP8X4 = mybir.dt.float8_e4m3fn_x4
GELU = mybir.ActivationFunctionType.Gelu_apprx_tanh

P = 128
PACK = 4
LINE = 4
STRIPE = 16
M_TILE = 128
PLANE = 4
EARLY = 384
SCALAR_PIECES = 4


def tile_picked_deform_lin_gelu_def_p_kernel(tc, x_words, x_scales, w, b, offs, out):
    nc = tc.nc
    with ExitStack() as ctx:
        keep = ctx.enter_context(tc.tile_pool(name="keep", bufs=1))
        psum = ctx.enter_context(tc.psum_pool(name="psum", bufs=1))

        offsets = keep.tile([P, TAPS * V // STRIPE], U16, name="offsets")
        nc.sync.dma_start(offsets[:], offs)

        pieces = [(0, 0, 256), (1, 0, 256), (2, 0, 256), (0, 256, 256), (1, 256, 128), (2, 256, 128), (1, 384, 128), (2, 384, 128)]
        raw = [keep.tile([P, PACK, width], F32, name=f"raw{i}") for i, (d, m0, width) in enumerate(pieces)]

        def load_piece(i):
            d, m0, width = pieces[i]
            nc.sync.dma_start(raw[i][:], w[d].rearrange("(p j) m -> p j m", j=PACK)[:, :, m0 : m0 + width])

        word_table = keep.tile([P, T], U32, name="word_table", align_bytes=64)
        words_in = x_words[0].rearrange("p n t -> p (n t)")

        def load_words(c0, c1):
            nc.sync.dma_start(word_table[:, c0:c1].bitcast(I32), words_in[:, PACK * c0 : PACK * c1].bitcast(I32))

        scale_table = keep.tile([P, T], U8, name="scale_table", align_bytes=64)
        nc.vector.memset(scale_table[:].bitcast(I32), 0)
        warm = keep.tile([P, 2], F32, name="warm")
        nc.gpsimd.memset(warm[:, 0:1], 0.0)
        nc.scalar.activation(warm[:, 1:2], warm[:, 0:1], GELU)
        bias_rows = keep.tile([P, P], F32, name="bias_rows")
        nc.gpsimd.memset(bias_rows[:], 0.0)
        load_piece(0)
        nc.sync.dma_start(scale_table[0:P:8, :].bitcast(I32), x_scales[0].bitcast(I32))
        nc.sync.dma_start(bias_rows[0 : M // M_TILE, :], b.rearrange("(t p) o -> t (p o)", p=P))
        load_words(0, 8 * EARLY)
        load_words(8 * EARLY, T)

        ident = keep.tile([P, P], F32, name="ident")
        make_identity(nc, ident[:])
        for i in range(1, len(pieces)):
            load_piece(i)

        x_codes = keep.tile([P, TAPS * V], U32, name="x_codes", align_bytes=64)
        picked_bytes = keep.tile([P, TAPS * V], U8, name="picked_bytes", align_bytes=64)
        x_bytes = keep.tile([P, TAPS * V], U8, name="x_bytes", align_bytes=64)
        nc.gpsimd.memset(x_bytes[:].bitcast(I32), 0)

        def gather(dst, table, e0, e1, cols):
            nc.vector.tensor_copy(dst[:, e0:e1], table[:, 0:cols].indirect(offsets[:, e0 // STRIPE : e1 // STRIPE]))

        w_codes = keep.tile([P, TAPS * M], U32, name="w_codes", align_bytes=64)
        w_bytes = keep.tile([P, TAPS * M], U8, name="w_bytes", align_bytes=64)
        groups = [(t, v0, V // 2) for v0 in (0, V // 2) for t in range(M // M_TILE)]
        ys = [keep.tile([P, V], F32, name=f"y{t}") for t in range(M // M_TILE)]
        grouped = [keep.tile([P, width, PACK], BF16, name=f"grouped{i}", align_bytes=64) for i, (d, m0, width) in enumerate(pieces)]

        def cast(i):
            dst = grouped[i][:].rearrange("p (c i) t -> p c t i", i=LINE)
            src = raw[i][:].rearrange("p t (c i) -> p c t i", i=LINE)
            if i < SCALAR_PIECES:
                nc.scalar.copy(dst, src)
            else:
                nc.vector.tensor_copy(dst, src)

        def quantize(i):
            d, m0, width = pieces[i]
            cols = slice(d * M + m0, d * M + m0 + width)
            nc.vector.quantize_mx(
                out=w_codes[:, cols].bitcast(FP8X4),
                scales=w_bytes[:, cols],
                in_=grouped[i][:].rearrange("p m t -> p (m t)"),
            )

        def multiply(i):
            d, m0, width = pieces[i]
            for g, (t, v0, n) in sorted(enumerate(groups), key=lambda e: e[1] if d > 0 else e[0]):
                if not m0 <= t * M_TILE < m0 + width:
                    continue
                mc = slice(d * M + t * M_TILE, d * M + (t + 1) * M_TILE)
                vc = slice(d * V + v0, d * V + v0 + n)
                nc.tensor.matmul_mx(
                    out=acc[g][:],
                    lhsT=w_codes[:, mc].bitcast(FP8X4),
                    lhsT_scale=w_bytes[:, mc],
                    rhs=x_codes[:, vc].bitcast(FP8X4),
                    rhs_scale=x_bytes[PLANE:P, vc],
                    start=(d == 0),
                    stop=(d == TAPS - 1),
                )
                if d == TAPS - 1:
                    y = ys[t]
                    nc.scalar.activation(y[:, v0 : v0 + n], acc[g][:], GELU, bias=bias[:, t : t + 1])
                    if t == M // M_TILE - 1:
                        nc.sync.dma_start(out[t * M_TILE : (t + 1) * M_TILE, v0 : v0 + n], y[:, v0 : v0 + n])
                    elif v0 > 0:
                        nc.sync.dma_start(out[t * M_TILE : (t + 1) * M_TILE, :], y[:])

        bias_ps = psum.tile([P, P], F32, name="bias_ps", tag="acc7")
        nc.tensor.transpose(bias_ps[:], bias_rows[:], ident[:])
        bias = keep.tile([P, M // M_TILE], F32, name="bias")
        nc.scalar.copy(bias[:], bias_ps[:, 0 : M // M_TILE])
        acc = [psum.tile([P, g[2]], F32, name=f"acc{i}", tag=f"acc{i}") for i, g in enumerate(groups)]

        cast(0)
        gather(picked_bytes, scale_table, 0, TAPS * V, T)
        for r in range(4):
            nc.scalar.dma_start(x_bytes[PLANE + r : P : 32, :].bitcast(I32), picked_bytes[8 * r : P : 32, :].bitcast(I32))
        quantize(0)
        gather(x_codes, word_table, 0, EARLY, 8 * EARLY)
        gather(x_codes, word_table, EARLY, EARLY + V, T)
        gather(x_codes, word_table, EARLY + V, 3 * V, T)
        multiply(0)

        cast(1)
        for i in range(2, len(pieces)):
            cast(i)
            quantize(i - 1)
            multiply(i - 1)
        quantize(len(pieces) - 1)
        multiply(len(pieces) - 1)
